import numpy as np
import ml_dtypes


def mxq(x, axis, fmt="e4m3"):
    dtype, down = {"e4m3": (ml_dtypes.float8_e4m3fn, 7), "e5m2": (ml_dtypes.float8_e5m2, 14)}[fmt]
    v = np.moveaxis(np.asarray(x, np.float32).astype(ml_dtypes.bfloat16).astype(np.float64), axis, -1)
    blocks = v.reshape(v.shape[:-1] + (-1, 32))
    amax = np.abs(blocks).max(-1, keepdims=True)
    byte = np.maximum(np.where(amax > 0, np.frexp(amax)[1] - 1 + 127, 0) - down, 1)
    scale = np.exp2(byte - 127.0)
    codes = (blocks / scale).astype(np.float32).astype(dtype).astype(np.float64)
    return np.moveaxis((codes * scale).reshape(v.shape), -1, axis)


WIDE = False


def mx_kscale(k):
    if not WIDE:
        return np.ones(k)
    levels = np.array([30, -30])
    if k % 512:
        return np.exp2(np.random.permutation(np.resize(levels, k // 32))).repeat(32)
    a = np.empty((k // 512, 16))
    for p in range(k // 512):
        a[p, :8] = np.random.permutation(np.resize(levels, 8))
        for g in range(8):
            far = levels[np.abs(levels - a[p, g]) >= 10]
            a[p, g + 8] = far[np.random.randint(len(far))]
    return np.exp2(a.ravel()).repeat(32)


def f64(x):
    return np.asarray(x).astype(np.float64)


def striped(idx):
    return np.tile(np.asarray(idx).reshape(-1, 16).T, (8, 1)).astype(np.uint16)


def unstriped(offs):
    return offs[:16].T.reshape(-1).astype(np.int64)


def striped8(idx):
    return np.asarray(idx).reshape(8, -1, 16).transpose(0, 2, 1).reshape(128, -1).astype(np.uint16)


def unstriped8(offs):
    return offs.reshape(8, 16, -1).transpose(0, 2, 1).reshape(8, -1).astype(np.int64)


def pick8(x, idx, run):
    r = np.arange(len(x))
    return x[r[:, None], idx[r % (8 * run) // run]]


E2M1 = np.array([0.0, 0.5, 1.0, 1.5, 2.0, 3.0, 4.0, 6.0, -0.0, -0.5, -1.0, -1.5, -2.0, -3.0, -4.0, -6.0])


def pack_weight(w, fmt):
    k, n = w.shape
    w = f64(np.asarray(w, np.float32).astype(ml_dtypes.bfloat16)).reshape(k // 32, 32, n)
    amax = np.abs(w).max(1)
    if fmt in ("e4m3", "e5m2"):
        byte = np.frexp(amax)[1] - 1 + 127 - (7 if fmt == "e4m3" else 14)
    else:
        mant, ex = np.frexp(amax / 6.0)
        byte = np.where(mant > 0.5, ex, ex - 1) + 127
    byte = np.clip(np.where(amax > 0, byte, 1), 1, 254)
    scaled = (w * np.exp2(127.0 - byte)[:, None, :]).reshape(k, n).astype(np.float32)
    by_word = np.ascontiguousarray(scaled.reshape(k // 512, 128, 4, n).transpose(0, 1, 3, 2))
    if fmt in ("e4m3", "e5m2"):
        words = by_word.astype(ml_dtypes.float8_e4m3fn if fmt == "e4m3" else ml_dtypes.float8_e5m2).view(np.uint8)
    else:
        c = by_word.astype(ml_dtypes.float4_e2m1fn).view(np.uint8) & 0xF
        words = (c[..., 0::2] | (c[..., 1::2] << 4)).reshape(k // 512, 128, 2 * n)
    return np.ascontiguousarray(words), np.ascontiguousarray(byte.astype(np.uint8).reshape(k // 512, 16, n))


def unpack_weight(words, scales, fmt):
    g, _, n = scales.shape
    words = np.ascontiguousarray(words).reshape(g, 128, n, -1)
    if fmt in ("e4m3", "e5m2"):
        vals = words.view(ml_dtypes.float8_e4m3fn if fmt == "e4m3" else ml_dtypes.float8_e5m2).astype(np.float64)
    else:
        nib = np.empty((g, 128, n, 4), np.uint8)
        nib[..., 0::2] = words & 0xF
        nib[..., 1::2] = words >> 4
        vals = E2M1[nib]
    vals = vals * np.repeat(np.exp2(scales.astype(np.float64) - 127.0), 8, axis=1)[..., None]
    return vals.transpose(0, 1, 3, 2).reshape(g * 512, n)


K, T, J, R, F, Z, C, O, N, E = 512, 1024, 256, 512, 512, 1024, 512, 128, 256, 512


def setup_inputs():
    n = np.random.standard_normal
    idx = np.random.permutation(T)[:J]
    idx2 = np.random.permutation(Z)[:J]
    idx3 = np.stack([np.random.permutation(C)[:J] for _ in range(8)])
    idx4 = np.random.permutation(C)[:O]
    idx5 = np.random.permutation(J)[:O]
    idx6 = np.random.permutation(E)[:O]
    idx7 = np.random.permutation(E)[:O]
    fk = mx_kscale(K)
    ff = mx_kscale(F)
    fr = mx_kscale(R)
    xtp = pack_weight(n((K, T)) / fk[:, None], "e2m1")
    xop = pack_weight(n((F, Z)) / ff[:, None], "e5m2")
    wp = pack_weight(n((K, R)) * 1 / np.sqrt(K) * fk[:, None] * fr, "e5m2")
    w2p = pack_weight(n((K, R)) * 1 / np.sqrt(K) * fk[:, None], "e4m3")
    w0p = pack_weight(n((F, R)) * 1 / np.sqrt(F) * ff[:, None], "e4m3")
    wbp = pack_weight(n((R, N)) * 1 / np.sqrt(R) / fr[:, None], "e4m3")
    return {
        "xt_words": xtp[0],
        "xt_scales": xtp[1],
        "xo_words": xop[0],
        "xo_scales": xop[1],
        "w_words": wp[0],
        "w_scales": wp[1],
        "w2_words": w2p[0],
        "w2_scales": w2p[1],
        "w0_words": w0p[0],
        "w0_scales": w0p[1],
        "wb_words": wbp[0],
        "wb_scales": wbp[1],
        "offs": striped(idx),
        "offs2": striped(idx2),
        "offs3": striped8(idx3),
        "offs4": striped(idx4),
        "offs5": striped(idx5),
        "offs6": striped(idx6),
        "offs7": striped(idx7),
    }


def reference(xt_words, xt_scales, xo_words, xo_scales, w_words, w_scales, w2_words, w2_scales, w0_words, w0_scales, wb_words, wb_scales, offs, offs2, offs3, offs4, offs5, offs6, offs7):
    idx = unstriped(offs)
    idx2 = unstriped(offs2)
    idx3 = unstriped8(offs3)
    idx4 = unstriped(offs4)
    idx5 = unstriped(offs5)
    idx6 = unstriped(offs6)
    idx7 = unstriped(offs7)
    xtu = unpack_weight(xt_words, xt_scales, "e2m1")
    xou = unpack_weight(xo_words, xo_scales, "e5m2")
    wu = unpack_weight(w_words, w_scales, "e5m2")
    w2u = unpack_weight(w2_words, w2_scales, "e4m3")
    w0u = unpack_weight(w0_words, w0_scales, "e4m3")
    wbu = unpack_weight(wb_words, wb_scales, "e4m3")
    xtidxg = xtu[:, idx]
    a = wu.T @ xtidxg
    xoidx2g = xou[:, idx2]
    b = w2u.T @ xtidxg + w0u.T @ xoidx2g
    lb = b[:, 0:1]
    la = a[:, 0:1]
    pw = np.zeros((R, C))
    pw[np.arange(R)[:, None], idx3[np.arange(R) % 512 // 64]] = a
    hid = np.maximum(pw[:, idx4] * lb, b[:, idx5] * la)
    hidq = mxq(hid, 0, "e5m2")
    p = wbu.T @ hidq
    pa = np.zeros((N, E))
    pa[:, idx6] = p
    pb = np.zeros((N, E))
    pb[:, idx7] = p
    y = pa + pb
    return y

@@ -1,0 +1,191 @@
+from contextlib import ExitStack
+
+import concourse.mybir as mybir
+
+K, T, J, R, F, Z, C, O, N, E = 512, 1024, 256, 512, 512, 1024, 512, 128, 256, 512
+FLOPS = 2 * (3 * K * R * J + R * N * O)
+
+F32 = mybir.dt.float32
+BF16 = mybir.dt.bfloat16
+I32 = mybir.dt.int32
+U32 = mybir.dt.uint32
+U16 = mybir.dt.uint16
+U8 = mybir.dt.uint8
+E4M3 = mybir.dt.float8_e4m3fn_x4
+E5M2 = mybir.dt.float8_e5m2_x4
+E2M1 = mybir.dt.float4_e2m1fn_x4
+COPY = mybir.ActivationFunctionType.Copy
+ALU = mybir.AluOpType
+
+P = 128
+PACK = 4
+LINE = 4
+
+
+def tile_list_ownlead_leaned_one_pagetwice_kernel(
+    tc, xt_words, xt_scales, xo_words, xo_scales, w_words, w_scales, w2_words, w2_scales,
+    w0_words, w0_scales, wb_words, wb_scales, offs, offs2, offs3, offs4, offs5, offs6, offs7, out,
+):
+    nc = tc.nc
+    with ExitStack() as ctx:
+        keep = ctx.enter_context(tc.tile_pool(name="keep", bufs=1))
+        psum = ctx.enter_context(tc.psum_pool(name="psum", bufs=1))
+
+        def load_list(name, src):
+            t = keep.tile(list(src.shape), U16, name=name)
+            nc.sync.dma_start(t[:], src)
+            return t
+
+        def zeroed_plane(name, width):
+            t = keep.tile([P, width], U8, name=name, align_bytes=64)
+            nc.vector.memset(t[:].bitcast(I32), 0)
+            return t
+
+        def load_plane(plane, scales):
+            for q in range(4):
+                nc.sync.dma_start(plane[32 * q : 32 * q + 4, :].bitcast(I32), scales[0, 4 * q : 4 * q + 4, :].bitcast(I32))
+
+        def load_words(name, words, width):
+            t = keep.tile([P, width], U32, name=name, align_bytes=64)
+            nc.sync.dma_start(t[:].bitcast(I32), words[0].rearrange("p n t -> p (n t)").bitcast(I32))
+            return t
+
+        def deal(name, raw, raw_plane, lo, hi, on_scalar):
+            words = keep.tile([P, (hi - lo) * P], U32, name=name + "_dealt", align_bytes=64)
+            plane = keep.tile([P, (hi - lo) * P], U8, name=name + "_dealt_plane", align_bytes=64)
+            nc.vector.tensor_copy(
+                plane[:].rearrange("p (t m) -> p t m", m=P),
+                raw_plane[:].rearrange("p (m t) -> p t m", t=PACK)[:, lo:hi, :],
+            )
+            move = nc.scalar.copy if on_scalar else nc.vector.tensor_copy
+            view = U32 if on_scalar else I32
+            move(
+                words[:].bitcast(view).rearrange("p (t c i) -> p c t i", t=hi - lo, i=LINE),
+                raw[:].bitcast(view).rearrange("p (c i t) -> p c t i", t=PACK, i=LINE)[:, :, lo:hi, :],
+            )
+            return words, plane
+
+        xt_plane = zeroed_plane("xt_plane", T)
+        w_plane = zeroed_plane("w_plane", R)
+        xo_plane = zeroed_plane("xo_plane", Z)
+        w2_plane = zeroed_plane("w2_plane", R)
+        w0_plane = zeroed_plane("w0_plane", R)
+        wb_plane = zeroed_plane("wb_plane", N)
+        boards = []
+        for t in range(PACK):
+            board = keep.tile([P, C], F32, name=f"board{t}", align_bytes=64)
+            nc.vector.memset(board[:], 0.0)
+            boards.append(board)
+
+        w_stage = keep.tile([4, 4, R // 4], I32, name="w_stage")
+        nc.sync.dma_start(w_stage[:], w_scales[0].bitcast(I32).rearrange("(q r) n -> r q n", r=4))
+        l1 = load_list("l1", offs)
+        load_plane(xt_plane, xt_scales)
+        xt_raw = keep.tile([P, T], U16, name="xt_raw", align_bytes=64)
+        nc.sync.dma_start(xt_raw[:].bitcast(I32), xt_words[0].bitcast(I32))
+        w_raw = load_words("w_raw", w_words, R)
+        l3 = load_list("l3", offs3)
+        l2 = load_list("l2", offs2)
+        load_plane(xo_plane, xo_scales)
+        xo_raw = load_words("xo_raw", xo_words, Z)
+        w2_raw = load_words("w2_raw", w2_words, R)
+        load_plane(w2_plane, w2_scales)
+        w0_raw = load_words("w0_raw", w0_words, R)
+        load_plane(w0_plane, w0_scales)
+        l4 = load_list("l4", offs4)
+        l5 = load_list("l5", offs5)
+        wb = load_words("wb", wb_words, N)
+        load_plane(wb_plane, wb_scales)
+        l6 = load_list("l6", offs6)
+        l7 = load_list("l7", offs7)
+
+        for q in range(4):
+            nc.vector.tensor_copy(w_plane[32 * q : 32 * q + 4, :].bitcast(I32), w_stage[:, q, :])
+        xt_g_plane = keep.tile([P, J], U8, name="xt_g_plane", align_bytes=64)
+        xt_g = keep.tile([P, J], U16, name="xt_g", align_bytes=64)
+        a = [keep.tile([P, J], F32, name=f"a{t}") for t in range(PACK)]
+        w_first, w_first_sc = deal("w_first", w_raw, w_plane, 0, 1, True)
+        for h in range(2):
+            js = slice(h * J // 2, (h + 1) * J // 2)
+            ls = slice(h * J // 32, (h + 1) * J // 32)
+            nc.vector.tensor_copy(xt_g_plane[:, js], xt_plane[:].indirect(l1[:, ls]))
+            nc.vector.tensor_copy(xt_g[:, js], xt_raw[:].indirect(l1[:, ls]))
+            acc = psum.tile([P, J // 2], F32, name=f"acc_a0{h}")
+            nc.tensor.matmul_mx(acc[:], lhsT=w_first[:].bitcast(E5M2), lhsT_scale=w_first_sc[:],
+                                rhs=xt_g[:, js].bitcast(E2M1), rhs_scale=xt_g_plane[:, js], start=True, stop=True)
+            if h == 0:
+                nc.scalar.activation(a[0][:, js], acc[:], COPY)
+            else:
+                nc.vector.tensor_copy(a[0][:, js], acc[:])
+            nc.scalar.activation(boards[0][:].indirect(l3[:, ls]), a[0][:, js], COPY)
+        w_rest, w_rest_sc = deal("w_rest", w_raw, w_plane, 1, PACK, True)
+        for t in range(1, PACK):
+            cols = slice(P * (t - 1), P * t)
+            acc = psum.tile([P, J], F32, name=f"acc_a{t}")
+            nc.tensor.matmul_mx(acc[:], lhsT=w_rest[:, cols].bitcast(E5M2), lhsT_scale=w_rest_sc[:, cols],
+                                rhs=xt_g[:].bitcast(E2M1), rhs_scale=xt_g_plane[:], start=True, stop=True)
+            nc.vector.tensor_copy(a[t][:], acc[:])
+            nc.scalar.activation(boards[t][:].indirect(l3[:]), a[t][:], COPY)
+
+        xo_g_plane = keep.tile([P, J], U8, name="xo_g_plane", align_bytes=64)
+        nc.vector.tensor_copy(xo_g_plane[:], xo_plane[:].indirect(l2[:]))
+        xo_g = keep.tile([P, J], U32, name="xo_g", align_bytes=64)
+        nc.vector.tensor_copy(xo_g[:], xo_raw[:].indirect(l2[:]))
+        w2, w2_sc = deal("w2", w2_raw, w2_plane, 0, PACK, False)
+        w0, w0_sc = deal("w0", w0_raw, w0_plane, 0, PACK, False)
+
+        look_board = keep.tile([P, PACK, O], F32, name="look_board")
+        look_b = keep.tile([P, PACK, O], F32, name="look_b")
+        b = []
+        for t in range(PACK):
+            cols = slice(P * t, P * (t + 1))
+            acc = psum.tile([P, J], F32, name=f"acc_b{t}", tag="acc_a00" if t == PACK - 1 else f"acc_b{t}")
+            nc.tensor.matmul_mx(acc[:], lhsT=w2[:, cols].bitcast(E4M3), lhsT_scale=w2_sc[:, cols],
+                                rhs=xt_g[:].bitcast(E2M1), rhs_scale=xt_g_plane[:], start=True, stop=False)
+            nc.tensor.matmul_mx(acc[:], lhsT=w0[:, cols].bitcast(E4M3), lhsT_scale=w0_sc[:, cols],
+                                rhs=xo_g[:].bitcast(E5M2), rhs_scale=xo_g_plane[:], start=False, stop=True)
+            bt = keep.tile([P, J], F32, name=f"b{t}")
+            nc.vector.tensor_copy(bt[:], acc[:])
+            nc.scalar.activation(look_board[:, t, :], boards[t][:].indirect(l4[:]), COPY, scale=bt[:, 0:1])
+            b.append(bt)
+        for t in range(PACK):
+            nc.scalar.activation(look_b[:, t, :], b[t][:].indirect(l5[:]), COPY, scale=a[t][:, 0:1])
+
+        pages = []
+        for u, tags in enumerate((("board0", "board1"), ("board2", "board3"))):
+            pair = []
+            for v, tag in enumerate(tags):
+                page = keep.tile([P, E], F32, name=f"page{u}{v}", tag=tag, align_bytes=64)
+                nc.vector.memset(page[:], 0.0)
+                pair.append(page)
+            pages.append(pair)
+
+        hid = keep.tile([P, O * PACK], BF16, name="hid", align_bytes=64)
+        nc.vector.tensor_tensor(
+            hid[:].rearrange("p (c i t) -> p c t i", t=PACK, i=LINE),
+            look_board[:].rearrange("p t (c i) -> p c t i", i=LINE),
+            look_b[:].rearrange("p t (c i) -> p c t i", i=LINE),
+            ALU.max,
+        )
+        hid_q = keep.tile([P, O], U32, name="hid_q", align_bytes=64)
+        hid_plane = keep.tile([P, O], U8, name="hid_plane", align_bytes=64)
+        nc.vector.quantize_mx(hid_q[:].bitcast(E5M2), hid_plane[:], hid[:])
+
+        ps = []
+        for u in range(2):
+            cols = slice(P * u, P * (u + 1))
+            acc = psum.tile([P, O], F32, name=f"acc_p{u}", tag=f"acc_a{u + 1}")
+            nc.tensor.matmul_mx(acc[:], lhsT=wb[:, cols].bitcast(E4M3), lhsT_scale=wb_plane[:, cols],
+                                rhs=hid_q[:].bitcast(E5M2), rhs_scale=hid_plane[:], start=True, stop=True)
+            pu = keep.tile([P, O], F32, name=f"p{u}")
+            if u == 0:
+                nc.vector.tensor_copy(pu[:], acc[:])
+            else:
+                nc.scalar.copy(pu[:], acc[:])
+            ps.append(pu)
+        for u in range(2):
+            nc.vector.tensor_copy(pages[u][0][:].indirect(l6[:]), ps[u][:])
+            nc.scalar.activation(pages[u][1][:].indirect(l7[:]), ps[u][:], COPY)
+            y = keep.tile([P, E], F32, name=f"y{u}")
+            nc.vector.tensor_tensor(y[:], pages[u][0][:], pages[u][1][:], ALU.add)
+            nc.sync.dma_start(out[P * u : P * (u + 1), :], y[:])

@@ -80,9 +80,9 @@ def tile_list_ownlead_leaned_one_pagetwice_kernel(
         w_stage = keep.tile([4, 4, R // 4], I32, name="w_stage")
         nc.sync.dma_start(w_stage[:], w_scales[0].bitcast(I32).rearrange("(q r) n -> r q n", r=4))
         l1 = load_list("l1", offs)
-        load_plane(xt_plane, xt_scales)
         xt_raw = keep.tile([P, T], U16, name="xt_raw", align_bytes=64)
         nc.sync.dma_start(xt_raw[:].bitcast(I32), xt_words[0].bitcast(I32))
+        load_plane(xt_plane, xt_scales)
         w_raw = load_words("w_raw", w_words, R)
         l3 = load_list("l3", offs3)
         l2 = load_list("l2", offs2)
@@ -108,8 +108,8 @@ def tile_list_ownlead_leaned_one_pagetwice_kernel(
         for h in range(2):
             js = slice(h * J // 2, (h + 1) * J // 2)
             ls = slice(h * J // 32, (h + 1) * J // 32)
-            nc.vector.tensor_copy(xt_g_plane[:, js], xt_plane[:].indirect(l1[:, ls]))
             nc.vector.tensor_copy(xt_g[:, js], xt_raw[:].indirect(l1[:, ls]))
+            nc.vector.tensor_copy(xt_g_plane[:, js], xt_plane[:].indirect(l1[:, ls]))
             acc = psum.tile([P, J // 2], F32, name=f"acc_a0{h}")
             nc.tensor.matmul_mx(acc[:], lhsT=w_first[:].bitcast(E5M2), lhsT_scale=w_first_sc[:],
                                 rhs=xt_g[:, js].bitcast(E2M1), rhs_scale=xt_g_plane[:, js], start=True, stop=True)
@@ -127,15 +127,14 @@ def tile_list_ownlead_leaned_one_pagetwice_kernel(
             nc.vector.tensor_copy(a[t][:], acc[:])
             nc.scalar.activation(boards[t][:].indirect(l3[:]), a[t][:], COPY)
 
-        xo_g_plane = keep.tile([P, J], U8, name="xo_g_plane", align_bytes=64)
+        xo_g_plane = keep.tile([P, J], U8, name="xo_g_plane", tag="w_rest_dealt_plane", align_bytes=64)
         nc.vector.tensor_copy(xo_g_plane[:], xo_plane[:].indirect(l2[:]))
-        xo_g = keep.tile([P, J], U32, name="xo_g", align_bytes=64)
+        xo_g = keep.tile([P, J], U32, name="xo_g", tag="w_rest_dealt", align_bytes=64)
         nc.vector.tensor_copy(xo_g[:], xo_raw[:].indirect(l2[:]))
         w2, w2_sc = deal("w2", w2_raw, w2_plane, 0, PACK, False)
         w0, w0_sc = deal("w0", w0_raw, w0_plane, 0, PACK, False)
 
         look_board = keep.tile([P, PACK, O], F32, name="look_board")
-        look_b = keep.tile([P, PACK, O], F32, name="look_b")
         b = []
         for t in range(PACK):
             cols = slice(P * t, P * (t + 1))
@@ -148,11 +147,9 @@ def tile_list_ownlead_leaned_one_pagetwice_kernel(
             nc.vector.tensor_copy(bt[:], acc[:])
             nc.scalar.activation(look_board[:, t, :], boards[t][:].indirect(l4[:]), COPY, scale=bt[:, 0:1])
             b.append(bt)
-        for t in range(PACK):
-            nc.scalar.activation(look_b[:, t, :], b[t][:].indirect(l5[:]), COPY, scale=a[t][:, 0:1])
 
         pages = []
-        for u, tags in enumerate((("board0", "board1"), ("board2", "board3"))):
+        for u, tags in enumerate((("w2_dealt", "board0"), ("board1", "board2"))):
             pair = []
             for v, tag in enumerate(tags):
                 page = keep.tile([P, E], F32, name=f"page{u}{v}", tag=tag, align_bytes=64)
@@ -160,32 +157,56 @@ def tile_list_ownlead_leaned_one_pagetwice_kernel(
                 pair.append(page)
             pages.append(pair)
 
-        hid = keep.tile([P, O * PACK], BF16, name="hid", align_bytes=64)
-        nc.vector.tensor_tensor(
-            hid[:].rearrange("p (c i t) -> p c t i", t=PACK, i=LINE),
-            look_board[:].rearrange("p t (c i) -> p c t i", i=LINE),
-            look_b[:].rearrange("p t (c i) -> p c t i", i=LINE),
-            ALU.max,
-        )
-        hid_q = keep.tile([P, O], U32, name="hid_q", align_bytes=64)
-        hid_plane = keep.tile([P, O], U8, name="hid_plane", align_bytes=64)
-        nc.vector.quantize_mx(hid_q[:].bitcast(E5M2), hid_plane[:], hid[:])
+        H = O // 2
+        hid_q = keep.tile([P, 3 * H], U32, name="hid_q", align_bytes=64)
+        hid_plane = keep.tile([P, 3 * H], U8, name="hid_plane", align_bytes=64)
+        nc.vector.memset(hid_q[:, H : 2 * H].bitcast(I32), 0)
+        nc.vector.memset(hid_plane[:, H : 2 * H].bitcast(I32), 0)
+        accs = []
+        for h in range(2):
+            os_ = slice(h * H, (h + 1) * H)
+            look_b = keep.tile([P, PACK, H], F32, name=f"look_b{h}", tag=("look_b0", "board3")[h], align_bytes=64)
+            for t in range(PACK):
+                nc.scalar.activation(look_b[:, t, :], b[t][:].indirect(l5[:, h * H // 16 : (h + 1) * H // 16]), COPY, scale=a[t][:, 0:1])
+            hid = keep.tile([P, H * PACK], BF16, name=f"hid{h}", tag="hid", align_bytes=64)
+            nc.vector.tensor_tensor(
+                hid[:].rearrange("p (c i t) -> p c t i", t=PACK, i=LINE),
+                look_board[:, :, os_].rearrange("p t (c i) -> p c t i", i=LINE),
+                look_b[:].rearrange("p t (c i) -> p c t i", i=LINE),
+                ALU.max,
+            )
+            made = slice(2 * h * H, (2 * h + 1) * H)
+            nc.vector.quantize_mx(hid_q[:, made].bitcast(E5M2), hid_plane[:, made], hid[:])
+            moving = slice(h * H, h * H + O)
+            for u in range(2):
+                cols = slice(P * u, P * (u + 1))
+                acc = psum.tile([P, O], F32, name=f"acc_p{h}{u}", tag=("acc_a01", "acc_a1", "acc_a2", "acc_a3")[2 * h + u])
+                nc.tensor.matmul_mx(acc[:], lhsT=wb[:, cols].bitcast(E4M3), lhsT_scale=wb_plane[:, cols],
+                                    rhs=hid_q[:, moving].bitcast(E5M2), rhs_scale=hid_plane[:, moving], start=True, stop=True)
+                accs.append(acc)
 
-        ps = []
-        for u in range(2):
-            cols = slice(P * u, P * (u + 1))
-            acc = psum.tile([P, O], F32, name=f"acc_p{u}", tag=f"acc_a{u + 1}")
-            nc.tensor.matmul_mx(acc[:], lhsT=wb[:, cols].bitcast(E4M3), lhsT_scale=wb_plane[:, cols],
-                                rhs=hid_q[:].bitcast(E5M2), rhs_scale=hid_plane[:], start=True, stop=True)
-            pu = keep.tile([P, O], F32, name=f"p{u}")
-            if u == 0:
-                nc.vector.tensor_copy(pu[:], acc[:])
+        def put(on_scalar, page, lst, src):
+            if on_scalar:
+                nc.scalar.activation(page[:].indirect(lst), src, COPY)
             else:
-                nc.scalar.copy(pu[:], acc[:])
-            ps.append(pu)
+                nc.vector.tensor_copy(page[:].indirect(lst), src)
+
+        for h in range(2):
+            ls = slice(h * H // 16, (h + 1) * H // 16)
+            ps = []
+            for u in range(2):
+                pu = keep.tile([P, H], F32, name=f"p{h}{u}", tag=f"p{u}")
+                src = accs[2 * h + u][:, h * H : (h + 1) * H]
+                if h == 1 and u == 0:
+                    nc.vector.tensor_copy(pu[:], src)
+                else:
+                    nc.scalar.copy(pu[:], src)
+                ps.append(pu)
+            for u in range(2):
+                put(h == 1 and u == 1, pages[u][0], l6[:, ls], ps[u][:])
+                put(True, pages[u][1], l7[:, ls], ps[u][:])
         for u in range(2):
-            nc.vector.tensor_copy(pages[u][0][:].indirect(l6[:]), ps[u][:])
-            nc.scalar.activation(pages[u][1][:].indirect(l7[:]), ps[u][:], COPY)
-            y = keep.tile([P, E], F32, name=f"y{u}")
-            nc.vector.tensor_tensor(y[:], pages[u][0][:], pages[u][1][:], ALU.add)
-            nc.sync.dma_start(out[P * u : P * (u + 1), :], y[:])
+            for es in ([slice(0, E)] if u == 0 else [slice(0, E // 2), slice(E // 2, E)]):
+                y = keep.tile([P, es.stop - es.start], F32, name=f"y{u}_{es.start}")
+                nc.vector.tensor_tensor(y[:], pages[u][0][:, es], pages[u][1][:, es], ALU.add)
+                nc.sync.dma_start(out[P * u : P * (u + 1), es], y[:])

@@ -77,13 +77,12 @@ def tile_list_ownlead_leaned_one_pagetwice_kernel(
             nc.vector.memset(board[:], 0.0)
             boards.append(board)
 
-        w_stage = keep.tile([4, 4, R // 4], I32, name="w_stage")
-        nc.sync.dma_start(w_stage[:], w_scales[0].bitcast(I32).rearrange("(q r) n -> r q n", r=4))
         l1 = load_list("l1", offs)
         xt_raw = keep.tile([P, T], U16, name="xt_raw", align_bytes=64)
-        nc.sync.dma_start(xt_raw[:].bitcast(I32), xt_words[0].bitcast(I32))
         load_plane(xt_plane, xt_scales)
+        nc.sync.dma_start(xt_raw[:].bitcast(I32), xt_words[0].bitcast(I32))
         w_raw = load_words("w_raw", w_words, R)
+        load_plane(w_plane, w_scales)
         l3 = load_list("l3", offs3)
         l2 = load_list("l2", offs2)
         load_plane(xo_plane, xo_scales)
@@ -99,33 +98,26 @@ def tile_list_ownlead_leaned_one_pagetwice_kernel(
         l6 = load_list("l6", offs6)
         l7 = load_list("l7", offs7)
 
-        for q in range(4):
-            nc.vector.tensor_copy(w_plane[32 * q : 32 * q + 4, :].bitcast(I32), w_stage[:, q, :])
         xt_g_plane = keep.tile([P, J], U8, name="xt_g_plane", align_bytes=64)
+        nc.vector.tensor_copy(xt_g_plane[:], xt_plane[:].indirect(l1[:]))
         xt_g = keep.tile([P, J], U16, name="xt_g", align_bytes=64)
-        a = [keep.tile([P, J], F32, name=f"a{t}") for t in range(PACK)]
-        w_first, w_first_sc = deal("w_first", w_raw, w_plane, 0, 1, True)
-        for h in range(2):
-            js = slice(h * J // 2, (h + 1) * J // 2)
-            ls = slice(h * J // 32, (h + 1) * J // 32)
-            nc.vector.tensor_copy(xt_g[:, js], xt_raw[:].indirect(l1[:, ls]))
-            nc.vector.tensor_copy(xt_g_plane[:, js], xt_plane[:].indirect(l1[:, ls]))
-            acc = psum.tile([P, J // 2], F32, name=f"acc_a0{h}")
-            nc.tensor.matmul_mx(acc[:], lhsT=w_first[:].bitcast(E5M2), lhsT_scale=w_first_sc[:],
-                                rhs=xt_g[:, js].bitcast(E2M1), rhs_scale=xt_g_plane[:, js], start=True, stop=True)
-            if h == 0:
-                nc.scalar.activation(a[0][:, js], acc[:], COPY)
-            else:
-                nc.vector.tensor_copy(a[0][:, js], acc[:])
-            nc.scalar.activation(boards[0][:].indirect(l3[:, ls]), a[0][:, js], COPY)
-        w_rest, w_rest_sc = deal("w_rest", w_raw, w_plane, 1, PACK, True)
-        for t in range(1, PACK):
-            cols = slice(P * (t - 1), P * t)
+        nc.vector.tensor_copy(xt_g[:], xt_raw[:].indirect(l1[:]))
+        w_first = deal("w_first", w_raw, w_plane, 0, 1, True)
+        w_rest = deal("w_rest", w_raw, w_plane, 1, PACK, True)
+        a = []
+        for t in range(PACK):
+            wt, wt_sc = w_first if t == 0 else w_rest
+            cols = slice(0, P) if t == 0 else slice(P * (t - 1), P * t)
             acc = psum.tile([P, J], F32, name=f"acc_a{t}")
-            nc.tensor.matmul_mx(acc[:], lhsT=w_rest[:, cols].bitcast(E5M2), lhsT_scale=w_rest_sc[:, cols],
+            nc.tensor.matmul_mx(acc[:], lhsT=wt[:, cols].bitcast(E5M2), lhsT_scale=wt_sc[:, cols],
                                 rhs=xt_g[:].bitcast(E2M1), rhs_scale=xt_g_plane[:], start=True, stop=True)
-            nc.vector.tensor_copy(a[t][:], acc[:])
-            nc.scalar.activation(boards[t][:].indirect(l3[:]), a[t][:], COPY)
+            at = keep.tile([P, J], F32, name=f"a{t}")
+            if t == 0:
+                nc.scalar.copy(at[:], acc[:])
+            else:
+                nc.vector.tensor_copy(at[:], acc[:])
+            nc.scalar.activation(boards[t][:].indirect(l3[:]), at[:], COPY)
+            a.append(at)
 
         xo_g_plane = keep.tile([P, J], U8, name="xo_g_plane", tag="w_rest_dealt_plane", align_bytes=64)
         nc.vector.tensor_copy(xo_g_plane[:], xo_plane[:].indirect(l2[:]))
@@ -138,7 +130,7 @@ def tile_list_ownlead_leaned_one_pagetwice_kernel(
         b = []
         for t in range(PACK):
             cols = slice(P * t, P * (t + 1))
-            acc = psum.tile([P, J], F32, name=f"acc_b{t}", tag="acc_a00" if t == PACK - 1 else f"acc_b{t}")
+            acc = psum.tile([P, J], F32, name=f"acc_b{t}")
             nc.tensor.matmul_mx(acc[:], lhsT=w2[:, cols].bitcast(E4M3), lhsT_scale=w2_sc[:, cols],
                                 rhs=xt_g[:].bitcast(E2M1), rhs_scale=xt_g_plane[:], start=True, stop=False)
             nc.tensor.matmul_mx(acc[:], lhsT=w0[:, cols].bitcast(E4M3), lhsT_scale=w0_sc[:, cols],
@@ -180,7 +172,7 @@ def tile_list_ownlead_leaned_one_pagetwice_kernel(
             moving = slice(h * H, h * H + O)
             for u in range(2):
                 cols = slice(P * u, P * (u + 1))
-                acc = psum.tile([P, O], F32, name=f"acc_p{h}{u}", tag=("acc_a01", "acc_a1", "acc_a2", "acc_a3")[2 * h + u])
+                acc = psum.tile([P, O], F32, name=f"acc_p{h}{u}", tag=f"acc_a{2 * h + u}")
                 nc.tensor.matmul_mx(acc[:], lhsT=wb[:, cols].bitcast(E4M3), lhsT_scale=wb_plane[:, cols],
                                     rhs=hid_q[:, moving].bitcast(E5M2), rhs_scale=hid_plane[:, moving], start=True, stop=True)
                 accs.append(acc)

from contextlib import ExitStack

import concourse.mybir as mybir

K, T, J, R, F, Z, C, O, N, E = 512, 1024, 256, 512, 512, 1024, 512, 128, 256, 512
FLOPS = 2 * (3 * K * R * J + R * N * O)

F32 = mybir.dt.float32
BF16 = mybir.dt.bfloat16
I32 = mybir.dt.int32
U32 = mybir.dt.uint32
U16 = mybir.dt.uint16
U8 = mybir.dt.uint8
E4M3 = mybir.dt.float8_e4m3fn_x4
E5M2 = mybir.dt.float8_e5m2_x4
E2M1 = mybir.dt.float4_e2m1fn_x4
COPY = mybir.ActivationFunctionType.Copy
ALU = mybir.AluOpType

P = 128
PACK = 4
LINE = 4


def tile_list_ownlead_leaned_one_pagetwice_kernel(
    tc, xt_words, xt_scales, xo_words, xo_scales, w_words, w_scales, w2_words, w2_scales,
    w0_words, w0_scales, wb_words, wb_scales, offs, offs2, offs3, offs4, offs5, offs6, offs7, out,
):
    nc = tc.nc
    with ExitStack() as ctx:
        keep = ctx.enter_context(tc.tile_pool(name="keep", bufs=1))
        psum = ctx.enter_context(tc.psum_pool(name="psum", bufs=1))

        def load_list(name, src):
            t = keep.tile(list(src.shape), U16, name=name)
            nc.sync.dma_start(t[:], src)
            return t

        def zeroed_plane(name, width):
            t = keep.tile([P, width], U8, name=name, align_bytes=64)
            nc.vector.memset(t[:].bitcast(I32), 0)
            return t

        def load_plane(plane, scales):
            for q in range(4):
                nc.sync.dma_start(plane[32 * q : 32 * q + 4, :].bitcast(I32), scales[0, 4 * q : 4 * q + 4, :].bitcast(I32))

        def load_words(name, words, width):
            t = keep.tile([P, width], U32, name=name, align_bytes=64)
            nc.sync.dma_start(t[:].bitcast(I32), words[0].rearrange("p n t -> p (n t)").bitcast(I32))
            return t

        def deal(name, raw, raw_plane, lo, hi, on_scalar):
            words = keep.tile([P, (hi - lo) * P], U32, name=name + "_dealt", align_bytes=64)
            plane = keep.tile([P, (hi - lo) * P], U8, name=name + "_dealt_plane", align_bytes=64)
            nc.vector.tensor_copy(
                plane[:].rearrange("p (t m) -> p t m", m=P),
                raw_plane[:].rearrange("p (m t) -> p t m", t=PACK)[:, lo:hi, :],
            )
            move = nc.scalar.copy if on_scalar else nc.vector.tensor_copy
            view = U32 if on_scalar else I32
            move(
                words[:].bitcast(view).rearrange("p (t c i) -> p c t i", t=hi - lo, i=LINE),
                raw[:].bitcast(view).rearrange("p (c i t) -> p c t i", t=PACK, i=LINE)[:, :, lo:hi, :],
            )
            return words, plane

        xt_plane = zeroed_plane("xt_plane", T)
        w_plane = zeroed_plane("w_plane", R)
        xo_plane = zeroed_plane("xo_plane", Z)
        w2_plane = zeroed_plane("w2_plane", R)
        w0_plane = zeroed_plane("w0_plane", R)
        wb_plane = zeroed_plane("wb_plane", N)
        boards = []
        for t in range(PACK):
            board = keep.tile([P, C], F32, name=f"board{t}", align_bytes=64)
            nc.vector.memset(board[:], 0.0)
            boards.append(board)

        l1 = load_list("l1", offs)
        xt_raw = keep.tile([P, T], U16, name="xt_raw", align_bytes=64)
        load_plane(xt_plane, xt_scales)
        nc.sync.dma_start(xt_raw[:].bitcast(I32), xt_words[0].bitcast(I32))
        w_raw = load_words("w_raw", w_words, R)
        load_plane(w_plane, w_scales)
        l3 = load_list("l3", offs3)
        l2 = load_list("l2", offs2)
        load_plane(xo_plane, xo_scales)
        xo_raw = load_words("xo_raw", xo_words, Z)
        w2_raw = load_words("w2_raw", w2_words, R)
        load_plane(w2_plane, w2_scales)
        w0_raw = load_words("w0_raw", w0_words, R)
        load_plane(w0_plane, w0_scales)
        l4 = load_list("l4", offs4)
        l5 = load_list("l5", offs5)
        wb = load_words("wb", wb_words, N)
        load_plane(wb_plane, wb_scales)
        l6 = load_list("l6", offs6)
        l7 = load_list("l7", offs7)

        xt_g_plane = keep.tile([P, J], U8, name="xt_g_plane", align_bytes=64)
        nc.vector.tensor_copy(xt_g_plane[:], xt_plane[:].indirect(l1[:]))
        xt_g = keep.tile([P, J], U16, name="xt_g", align_bytes=64)
        nc.vector.tensor_copy(xt_g[:], xt_raw[:].indirect(l1[:]))
        w_first = deal("w_first", w_raw, w_plane, 0, 1, True)
        w_rest = deal("w_rest", w_raw, w_plane, 1, PACK, True)
        a = []
        for t in range(PACK):
            wt, wt_sc = w_first if t == 0 else w_rest
            cols = slice(0, P) if t == 0 else slice(P * (t - 1), P * t)
            acc = psum.tile([P, J], F32, name=f"acc_a{t}")
            nc.tensor.matmul_mx(acc[:], lhsT=wt[:, cols].bitcast(E5M2), lhsT_scale=wt_sc[:, cols],
                                rhs=xt_g[:].bitcast(E2M1), rhs_scale=xt_g_plane[:], start=True, stop=True)
            at = keep.tile([P, J], F32, name=f"a{t}")
            if t == 0:
                nc.scalar.copy(at[:], acc[:])
            else:
                nc.vector.tensor_copy(at[:], acc[:])
            nc.scalar.activation(boards[t][:].indirect(l3[:]), at[:], COPY)
            a.append(at)

        xo_g_plane = keep.tile([P, J], U8, name="xo_g_plane", tag="w_rest_dealt_plane", align_bytes=64)
        nc.vector.tensor_copy(xo_g_plane[:], xo_plane[:].indirect(l2[:]))
        xo_g = keep.tile([P, J], U32, name="xo_g", tag="w_rest_dealt", align_bytes=64)
        nc.vector.tensor_copy(xo_g[:], xo_raw[:].indirect(l2[:]))
        w2, w2_sc = deal("w2", w2_raw, w2_plane, 0, PACK, False)
        w0, w0_sc = deal("w0", w0_raw, w0_plane, 0, PACK, False)

        look_board = keep.tile([P, PACK, O], F32, name="look_board")
        b = []
        for t in range(PACK):
            cols = slice(P * t, P * (t + 1))
            acc = psum.tile([P, J], F32, name=f"acc_b{t}")
            nc.tensor.matmul_mx(acc[:], lhsT=w2[:, cols].bitcast(E4M3), lhsT_scale=w2_sc[:, cols],
                                rhs=xt_g[:].bitcast(E2M1), rhs_scale=xt_g_plane[:], start=True, stop=False)
            nc.tensor.matmul_mx(acc[:], lhsT=w0[:, cols].bitcast(E4M3), lhsT_scale=w0_sc[:, cols],
                                rhs=xo_g[:].bitcast(E5M2), rhs_scale=xo_g_plane[:], start=False, stop=True)
            bt = keep.tile([P, J], F32, name=f"b{t}")
            nc.vector.tensor_copy(bt[:], acc[:])
            nc.scalar.activation(look_board[:, t, :], boards[t][:].indirect(l4[:]), COPY, scale=bt[:, 0:1])
            b.append(bt)

        pages = []
        for u, tags in enumerate((("w2_dealt", "board0"), ("board1", "board2"))):
            pair = []
            for v, tag in enumerate(tags):
                page = keep.tile([P, E], F32, name=f"page{u}{v}", tag=tag, align_bytes=64)
                nc.vector.memset(page[:], 0.0)
                pair.append(page)
            pages.append(pair)

        H = O // 2
        hid_q = keep.tile([P, 3 * H], U32, name="hid_q", align_bytes=64)
        hid_plane = keep.tile([P, 3 * H], U8, name="hid_plane", align_bytes=64)
        nc.vector.memset(hid_q[:, H : 2 * H].bitcast(I32), 0)
        nc.vector.memset(hid_plane[:, H : 2 * H].bitcast(I32), 0)
        accs = []
        for h in range(2):
            os_ = slice(h * H, (h + 1) * H)
            look_b = keep.tile([P, PACK, H], F32, name=f"look_b{h}", tag=("look_b0", "board3")[h], align_bytes=64)
            for t in range(PACK):
                nc.scalar.activation(look_b[:, t, :], b[t][:].indirect(l5[:, h * H // 16 : (h + 1) * H // 16]), COPY, scale=a[t][:, 0:1])
            hid = keep.tile([P, H * PACK], BF16, name=f"hid{h}", tag="hid", align_bytes=64)
            nc.vector.tensor_tensor(
                hid[:].rearrange("p (c i t) -> p c t i", t=PACK, i=LINE),
                look_board[:, :, os_].rearrange("p t (c i) -> p c t i", i=LINE),
                look_b[:].rearrange("p t (c i) -> p c t i", i=LINE),
                ALU.max,
            )
            made = slice(2 * h * H, (2 * h + 1) * H)
            nc.vector.quantize_mx(hid_q[:, made].bitcast(E5M2), hid_plane[:, made], hid[:])
            moving = slice(h * H, h * H + O)
            for u in range(2):
                cols = slice(P * u, P * (u + 1))
                acc = psum.tile([P, O], F32, name=f"acc_p{h}{u}", tag=f"acc_a{2 * h + u}")
                nc.tensor.matmul_mx(acc[:], lhsT=wb[:, cols].bitcast(E4M3), lhsT_scale=wb_plane[:, cols],
                                    rhs=hid_q[:, moving].bitcast(E5M2), rhs_scale=hid_plane[:, moving], start=True, stop=True)
                accs.append(acc)

        def put(on_scalar, page, lst, src):
            if on_scalar:
                nc.scalar.activation(page[:].indirect(lst), src, COPY)
            else:
                nc.vector.tensor_copy(page[:].indirect(lst), src)

        for h in range(2):
            ls = slice(h * H // 16, (h + 1) * H // 16)
            ps = []
            for u in range(2):
                pu = keep.tile([P, H], F32, name=f"p{h}{u}", tag=f"p{u}")
                src = accs[2 * h + u][:, h * H : (h + 1) * H]
                if h == 1 and u == 0:
                    nc.vector.tensor_copy(pu[:], src)
                else:
                    nc.scalar.copy(pu[:], src)
                ps.append(pu)
            for u in range(2):
                put(h == 1 and u == 1, pages[u][0], l6[:, ls], ps[u][:])
                put(True, pages[u][1], l7[:, ls], ps[u][:])
        for u in range(2):
            for es in ([slice(0, E)] if u == 0 else [slice(0, E // 2), slice(E // 2, E)]):
                y = keep.tile([P, es.stop - es.start], F32, name=f"y{u}_{es.start}")
                nc.vector.tensor_tensor(y[:], pages[u][0][:, es], pages[u][1][:, es], ALU.add)
                nc.sync.dma_start(out[P * u : P * (u + 1), es], y[:])
